import numpy as np, ml_dtypes
CORES = [5,29,101,125,133,157,229,253]
N = 8
BF = ml_dtypes.bfloat16
def gentries(a):
    return np.ascontiguousarray(a.reshape(8, 16, -1).transpose(0, 2, 1)).reshape(8, -1)
def gtable(e):
    e = np.asarray(e); return np.ascontiguousarray(e.reshape(8, -1, 16).transpose(0, 2, 1)).reshape(128, -1).astype(np.int32)
V, G, CAP, RO = 768, 256, 256, 4
W = V + (N - 1) * G + 17
H = 16 - RO
def parts(rng):
    h = V // 2; S = (N, 8, 16, V)
    o = np.argsort(rng.random(S), axis=-1); a, b = o[..., :h], o[..., h:]
    pool = np.concatenate([b, np.broadcast_to(np.arange(V, W), (N, 8, 16, W - V))], axis=-1)
    pool = np.take_along_axis(pool, np.argsort(rng.random(pool.shape), axis=-1), -1)[..., :V - h]
    nb = np.zeros(S, np.int64)
    np.put_along_axis(nb, o, np.concatenate([a.reshape(N, 8, 16, h // 2, 2)[..., ::-1].reshape(N, 8, 16, h), pool], axis=-1), -1)
    share = rng.permutation(np.array([0.003, 0.003, 0.01, 0.02, 0.05, 0.1, 0.3, 0.6])).reshape(1, 8, 1, 1) * np.exp2(rng.integers(-1, 2, (N, 8, 1, 1)))
    m = (rng.random((N, 8, 1, V)) < share) & (rng.random(S) < 0.5)
    d0 = np.where(m, rng.integers(0, 201, S), 255); nd = rng.integers(1, 64, S); e = rng.random(S)
    lab = np.where(e < 0.3, W - 1, np.where(e < 0.5, rng.integers(W - 17, W - 1, S), rng.integers(0, W - 17, S)))
    hi = rng.permuted(np.tile(np.array([8, 16, 32, 64, 96, 128, 192, 256]), (N, 1)), axis=1).reshape(N, 8, 1, 1)
    ld = (rng.random(S) * hi).astype(np.int64)
    rt = rng.integers(20, 181, (8, 16, 16)); rt[:, np.arange(16), np.arange(16)] = 0; rt = np.tile(rt, (N, 1, 1, 1))
    p = rng.permuted(np.tile(np.array([0.03, 0.05, 0.1, 0.15, 0.2, 0.3, 0.5, 1.0]), (N, 1)), axis=1).reshape(N, 8, 1)
    fl = (rng.random((N, 8, V)) < p).astype(np.int64)
    snd = np.ascontiguousarray(np.argsort(rng.random((N, 8, N - 1, V)), axis=-1)[..., :G])
    return nb, nd, lab, ld, d0, rt, fl, snd
def flat(a, t):
    return np.ascontiguousarray(a.reshape(N, 128, -1)).astype(np.float32).astype(t)
def pack(nb, nd, lab, ld, d0, rt, fl, snd):
    lab = np.array(lab); ld = np.array(ld); lab[:, :, H:] = W - 1; ld[:, :, H:] = 255
    return {"nb": flat(nb, np.int32), "nd": flat(nd, BF), "lab": flat(lab, np.int32), "ld": flat(ld, BF), "d0": flat(d0, BF), "rt": flat(rt, BF),
            "fl": fl.astype(np.int32), "snd": np.stack([gtable(a.reshape(8, -1)) for a in snd])}
def put(row, j, p):
    old = int(row[j]); row[row == p] = old; row[j] = p
def load(rng, nq, nl, lq, dq, fq, sq):
    s = np.nonzero(fq)[0][:CAP]; t = rng.permutation(np.setdiff1d(np.arange(V), s)); T = (N - 1) * G
    sq[:] = rng.permutation(np.concatenate([rng.permutation(s), t])[:G])
    nq[0, s] = t[:CAP]; nq[0, t] = rng.permutation(np.concatenate([t[CAP:], s])); gp = V + rng.permutation(T)
    for i in range(1, 16):
        p = gp[(np.arange(CAP) + (i - 1) * CAP) % T]
        nq[i, s] = p; nq[i, t] = rng.permutation(np.setdiff1d(np.arange(W), p))[:V - CAP]
    nl[:, s] = rng.integers(1, 50, (16, CAP)); lq[:] = W - 1
    dq[:] = 255; dq[:, t[:CAP]] = rng.integers(0, 101, (16, CAP))
def setup_inputs(rng):
    return pack(*parts(rng))
def setup_inputs_room(rng):
    nb, nd, lab, ld, d0, rt, fl, snd = parts(rng); fl[:] = 0
    for q in range(N):
        full = q >= max(1, N // 4)
        for g in range(8):
            n = int(rng.choice(np.array([CAP, CAP + 1, V] if full else [0, 1, CAP - 1, CAP, CAP + 1, V])))
            if q == 0: n = (CAP, CAP + 1, CAP - 1, V, 0, 1, CAP, CAP + 1)[g]
            fl[q, g, rng.permutation(V)[:n]] = 1
            if full: load(rng, nb[q, g], nd[q, g], lab[q, g], d0[q, g], fl[q, g], snd[q, g])
    c = snd[0, 0, 0]; isin = np.zeros(V, np.int64); isin[c] = 1
    o = np.concatenate([rng.permutation(c), rng.permutation(np.nonzero(isin == 0)[0])])
    s, t = o[:CAP], rng.permutation(o[CAP:])
    fl[0, 0] = 0; fl[0, 0, s] = 1
    nb[0, 0, 0, s] = t[:CAP]; nb[0, 0, 0, t] = rng.permutation(np.concatenate([t[CAP:], s]))
    nd[0, 0][:, s] = rng.integers(1, 50, (16, CAP)); lab[0, 0][:, s] = W - 1
    d0[0, 0][:, s] = 255; d0[0, 0][:, t[:CAP]] = rng.integers(0, 101, (16, CAP))
    return pack(nb, nd, lab, ld, d0, rt, fl, snd)
def setup_inputs_ties(rng):
    nb, nd, lab, ld, d0, rt, fl, snd = parts(rng); S = (N, 8, 16, V)
    base = np.array([0, 0, 1, 4, 250, 251, 252, 252]).reshape(1, 8, 1, 1); share = np.array([0.3, 0.1, 0.02, 0.3, 0.02, 0.02, 0.01, 0.005]).reshape(1, 8, 1, 1)
    m = (rng.random((N, 8, 1, V)) < share) & (rng.random(S) < 0.6)
    d0 = np.where(m, base + rng.integers(0, 4, S), 255); nd = rng.integers(0, 3, S); ld = rng.integers(0, 4, S)
    rt = np.minimum(base + rng.integers(0, 5, (N, 8, 16, 16)), 255)
    return pack(nb, nd, lab, ld, d0, rt, fl, snd)
def setup_inputs_alike(rng):
    nb, nd, lab, ld, d0, rt, fl, snd = parts(rng)
    q = int(rng.integers(0, N)); o = rng.permutation(CAP)[:12]; u, x = o[:4], o[4:8]
    for a in range(N):
        d = (a - q) % N; v = o[8:]; p = u
        if d > 0:
            v = rng.permutation(CAP)[:4]; sp = rng.permutation(G)[:4]; p = V + (d - 1) * G + sp
            for j in range(4): put(snd[q, 0, d - 1], sp[j], u[j])
        for j in range(4): put(nb[a, 0, 0], v[j], p[j])
        nd[a, 0][:, v] = rng.integers(1, 50, (16, 4)); lab[a, 0][:, v] = W - 1; d0[a, 0][:, v] = 255; fl[a, 0, v] = 1
    for j in range(4): put(nb[q, 0, 0], u[j], x[j])
    nd[q, 0][:, u] = rng.integers(1, 30, (16, 4)); lab[q, 0][:, u] = W - 1; fl[q, 0, u] = 0
    d0[q, 0][:, u] = rng.integers(60, 101, (16, 4)); d0[q, 0][:, x] = 0
    nb[:, 0] = np.array(nb[:, 0, :1]); nb[:, 1, 0] = np.arange(V); nb[:, 2] = W - 1 - np.arange(V); nb[:, 3] = np.arange(V, 2 * V)
    lab[:, 4] = rng.choice(np.array([0, V - 1, V, W - 18, W - 17, W - 2, W - 1]), (N, 16, V)); lab[:, 5] = np.array(lab[:, 5, :1])
    snd[:, 1::2] = np.array(snd[:, 1::2, :1])
    return pack(nb, nd, lab, ld, d0, rt, fl, snd)
def setup_inputs_quiet(rng):
    nb, nd, lab, ld, d0, rt, fl, snd = parts(rng)
    q = int(rng.integers(0, N)); g = rng.permutation(8); w = fl[q] * 1; fl[:] = 0; fl[q] = w
    fl[q, g[0]] = 0; fl[q, g[1]] = 0; fl[q, g[1], 0] = 1; fl[q, g[1], V - 1] = 1
    h = int(g[2]); fl[q, h] = 1
    for i in range(16):
        p = rng.permutation(CAP) if i == 0 else CAP + rng.permutation(V - CAP)[:CAP]
        nb[q, h, i, :CAP] = p; nb[q, h, i, CAP:] = rng.permutation(np.setdiff1d(np.arange(W), p))[:V - CAP]
    nd[q, h][:, :CAP] = 255; nd[q, h, 1, :CAP] = rng.integers(1, 50, CAP); lab[q, h][:, :CAP + 8] = W - 1
    d0[q, h][:, :CAP] = 255; d0[q, h][:, CAP:] = rng.integers(50, 101, (16, V - CAP)); d0[q, h][:, V - 8:] = 0
    for j in range(8): put(nb[q, h, 0], CAP + j, V - 8 + j)
    nd[q, h, 0, CAP:CAP + 8] = rng.integers(1, 30, 8)
    return pack(nb, nd, lab, ld, d0, rt, fl, snd)
def setup_inputs_spread(rng):
    nb, nd, lab, ld, d0, rt, fl, snd = parts(rng); S = (N, 8, 16, V)
    d0 = np.where(rng.random((N, 8, 1, V)) < 0.2, 255, np.minimum(np.exp2(8 * rng.random((N, 8, 1, V))) * (0.5 + rng.random(S)), 255).astype(np.int64))
    nd = np.minimum(np.exp2(8.1 * rng.random(S)).astype(np.int64) - (rng.random(S) < 0.5), 255)
    ld = np.minimum(np.exp2(8.1 * rng.random(S)).astype(np.int64), 255) * (rng.random(S) < 0.97)
    lab = rng.integers(0, W, S); rt = rng.integers(0, 256, (N, 8, 16, 16))
    fl = (rng.random((N, 8, V)) < rng.random((N, 8, 1)) * rng.random((N, 8, V))).astype(np.int64)
    return pack(nb, nd, lab, ld, d0, rt, fl, snd)
def check_inputs(d):
    bad = []
    for k, lo, hi in (("nb", 0, W - 1), ("lab", 0, W - 1), ("fl", 0, 1), ("snd", 0, V - 1)):
        if np.min(d[k]) < lo or np.max(d[k]) > hi: bad.append("range of " + k)
    for k in ("nd", "ld", "d0", "rt"):
        a = np.asarray(d[k]).astype(np.float32)
        if not np.all((a >= 0) & (a <= 255) & (a == np.floor(a))): bad.append("whole numbers from 0 to 255 in " + k)
    if np.any(np.diff(np.sort(np.asarray(d["nb"]), axis=-1), axis=-1) == 0): bad.append("nb: the numbers of one row differ")
    s = np.stack([gentries(a) for a in np.asarray(d["snd"])]).reshape(N, 8, N - 1, G)
    if np.any(np.diff(np.sort(s, axis=-1), axis=-1) == 0): bad.append("snd: the numbers of one block differ")
    if np.any(np.asarray(d["lab"]).reshape(N, 8, 16, V)[:, :, H:] != W - 1): bad.append("lab: the later entries are the none place")
    if np.any(np.asarray(d["ld"]).astype(np.float32).reshape(N, 8, 16, V)[:, :, H:] != 255): bad.append("ld: the later entries are 255")
    return bad
def ints(a):
    return np.asarray(a).astype(np.float32).astype(np.int64)
def reference(nb, nd, lab, ld, d0, rt, fl, snd):
    S = (N, 8, 16, V); nbl = ints(nb).reshape(S); ndl = ints(nd).reshape(S)
    L = np.array(ints(lab).reshape(S)); M = np.array(ints(ld).reshape(S)); D = np.array(ints(d0).reshape(S))
    R = ints(rt).reshape(N, 8, 16, 16); flag = ints(fl).reshape(N, 8, V) > 0
    sl = np.stack([gentries(a) for a in snd]).astype(np.int64).reshape(N, 8, N - 1, G)
    none = np.full((8, 16, 1), 255, np.int64)
    for t in range(RO):
        F = flag & (np.add.accumulate(flag.astype(np.int64), axis=2) <= CAP)
        flag = flag & ~F
        new = np.array(D); push = np.zeros((N, 8, W), bool)
        for a in range(N):
            guests = [np.take_along_axis(D[(a - d) % N], sl[(a - d) % N, :, d - 1][:, None, :], 2) for d in range(1, N)]
            win = np.concatenate([D[a]] + guests + [R[a], none], axis=2)
            for g in range(8):
                v = np.nonzero(F[a, g])[0]; w = win[g]; old = D[a, g][:, v]
                cand = np.minimum(np.min(w[:, nbl[a, g][:, v]] + ndl[a, g][:, v], axis=1), 255)
                q = np.minimum(np.min(w[:, L[a, g][:, v]] + M[a, g][:, v], axis=1), 255)
                up = (cand < q) & (cand < old); ch = np.any(up, axis=0)
                key = np.where(up, cand, 1000); best = np.argmin(key, axis=0); least = np.min(key, axis=0)
                new[a, g][:, v] = np.where(up, cand, old)
                L[a, g, H + t, v[ch]] = W - 17 + best[ch]; M[a, g, H + t, v[ch]] = least[ch]
                push[a, g, nbl[a, g][:, v[ch]]] = True
        D = new
        for a in range(N):
            flag[a] |= push[a, :, :V]
            for d in range(1, N):
                back = np.zeros((8, V), bool)
                np.put_along_axis(back, sl[(a - d) % N, :, d - 1], push[a, :, V + (d - 1) * G:V + d * G], 1)
                flag[(a - d) % N] |= back
    return {"yd": D.reshape(N, 128, V).astype(np.float32).astype(BF), "yl": L.reshape(N, 128, V).astype(np.float32)}

from concourse.bass import DstId, RemoteDMATransfer
from concourse.mybir import AluOpType, ActivationFunctionType

N, V, G, RO = 8, 768, 256, 4
W = V + (N - 1) * G + 17
WP = 2592
TG = N * V
BIG = 6176
LEV = [2.0 ** -9, 2.0 ** -4, 1.3]
THR = [0.75 * 2.0 ** -10, 0.75 * 2.0 ** -5, 0.75]
LAB_A = [112, 104, 104, 120]
NB_V = [16, 16, 16, 16]
Y_V = [32, 32, 32]
PUSH_A = 8
CMP_A = 24

SCRATCH = {}
for _d, _l in {
    "int32": dict(NBI=V, LABI=V, SNI=112, FLI=48, RL=112, pcol=4, vraw=48, vR=48, praw=16, pr2=16, t48a=48, t48b=48,
                  w0=16, w1=16, w2=16),
    "uint16": dict(SNU=112, RU=112, PERM=16, BC=16, POS=48, TL=16, LO=256, NO=256, PO=256),
    "float32": dict(YL=V, VSf=16 * CMP_A, CWf=V, stB=384, Wf=2 * BIG, CF=16, RM=16, B48=8, bcf=16, c1=48, c2=48, ZF=384,
                    VF=256, Fc=48, Sc=48, pre=48, RED=16, OS=256, TM=256, KS=256, w3=16, LA=256, LV=256),
    "bfloat16": dict(ND=V, LD=V, Dw0=WP, Dw1=WP, Dw2=WP, Dw3=WP, CM=WP, VS=V, CW=V, CWa=256, Gs0=1792, Gs1=1792, Gs2=1792,
                     Gs3=1792, FL0=384, FL1=384, FL2=384, SM0=384, SM1=384, SM2=384, stA=384, Wb=2 * BIG, Gl=4096, Gn=4096,
                     Y=4096, IJ=256, MG=128, q0=48, q1=48, q2=48, BLK=128, ID=128, LT=128, I5=128, I16=128, I8K=128, DK=128,
                     ONE=128, ZS=144, SI=2048, RS=256, ZL=272, ZD=272, ZB=384, VB=256, OLD=256, F=48, S=48, lf0=48, LEFT=48,
                     INV=256, LDT=256, NDT=256, aA=256, aB=256, CC=256, NU=256, n2=256, DV=256),
}.items():
    for _n, _c in _l.items():
        SCRATCH[_n] = ("sbuf", [128, _c], _d)
PSUM = ["s0", "s1", "s2", "s3", "pa", "pb", "pO", "pK"]
for _n in PSUM:
    SCRATCH[_n] = ("psum", [128, 512], "float32")
SEMAPHORES = ["qv", "qa", "qt", "qg", "ls", "ls0"] + ["arr%d" % m for m in range(8)] + ["dm%d" % m for m in range(44)]

A = AluOpType
AF = ActivationFunctionType


def mask_of(eng):
    m = 0
    for e in eng:
        m |= 1 << e
    return m


def in_calls(qs):
    out = []
    while qs:
        k = 1
        while 2 * k <= len(qs):
            k *= 2
        out.append(qs[:k])
        qs = qs[k:]
    return out


def routes(T, topo, r):
    me = T.cores[r]
    others = [(r + d) % N for d in range(1, N)]
    first = {q: T.cores[q] for q in others if topo.may_write(me, T.cores[q])}
    direct = list(first)
    relay = [q for q in others if q not in first]
    for q in relay:
        first[q] = [c for c in topo.cores_of(me)
                    if c not in T.cores and c not in first.values() and topo.may_write(c, T.cores[q])][0]
    out = {}
    for run in in_calls(direct) + in_calls(relay):
        eng = topo.engines(me, first[run[0]])
        k = len(eng) // len(run)
        for n, q in enumerate(run):
            out[q] = (first[q], eng[n * k:n * k + k])
    return out


def landing(T, m, src, dst):
    if m >= 2 and m % 2 == 0:
        d = (src - dst) % N
        return T["FL%d" % ((m - 2) // 2)][:, 48 * d:48 * d + 48]
    d = (dst - src) % N
    if m == 1:
        return T.RL[:, 16 * (d - 1):16 * d]
    return T["Dw%d" % (0 if m == 0 else (m - 1) // 2)][:, V + (d - 1) * G:V + d * G]


def helper_program(g, core, T, topo):
    for r in range(N):
        if core not in topo.cores_of(T.cores[r]):
            continue
        for q, (h, e) in routes(T, topo, r).items():
            if h != core:
                continue
            dst = T.cores[q]
            rid, pid = topo.addr(dst, core)
            k = len(topo.engines(core, dst))
            for m in [1, 0] + list(range(2, 8)):
                g.wait_ge(T.sem["arr%d" % m], len(e))
                ap = landing(T, m, r, q)
                g.remote_dma(ap, ap, T.sem["arr%d" % m], T.sem.ls, pid, rid, topo.mask(core, dst))
            g.wait_ge(T.sem.ls, 8 * k)


def rank_program(g, core, T, topo):
    rank = T.rank_of(core)
    if rank is None:
        helper_program(g, core, T, topo)
        return
    Q = {"v": g.vector, "a": g.scalar, "t": g.tensor, "g": g, "s": g.sync}
    cnt = {}
    waited = {q: {} for q in Q}
    lastw, readers = {}, {}
    ndma = [0]

    def need(q, ev, free):
        sem, c, eq, dma = ev
        if eq == q and not dma and free:
            return
        if waited[q].get(sem, 0) < c:
            Q[q].wait_ge(T.sem[sem], c)
            waited[q][sem] = c

    def deps(q, R, Wr):
        for k in R:
            if k in lastw:
                need(q, lastw[k], False)
        for k in Wr:
            if k in lastw:
                need(q, lastw[k], k in PSUM)
            for ev in readers.get(k, {}).values():
                need(q, ev, False)

    def done(ev, R, Wr):
        for k in R:
            readers.setdefault(k, {})[ev[0]] = ev
        for k in Wr:
            lastw[k] = ev
            readers[k] = {}

    def op(q, fn, R, Wr):
        deps(q, R, Wr)
        ins = fn()
        sem = "q" + q
        cnt[sem] = cnt.get(sem, 0) + 1
        ins.then_inc(T.sem[sem], 1)
        done((sem, cnt[sem], q, False), R, Wr)

    def dma(q, out, in_, R, Wr):
        deps(q, R, Wr)
        sem = "dm%d" % ndma[0]
        ndma[0] += 1
        cnt[sem] = 16
        Q[q].dma_start(out, in_).then_inc(T.sem[sem], 16)
        done((sem, 16, q, True), R, Wr)

    v, a, pe = g.vector, g.scalar, g.tensor

    def ts(out, in0, s1, o0, R, Wr, s2=None, o1=None):
        if o1 is None:
            op("v", lambda: v.tensor_scalar(out, in0, s1, None, o0), R, Wr)
        else:
            op("v", lambda: v.tensor_scalar(out, in0, s1, s2, o0, o1), R, Wr)

    def tt(out, in0, in1, o, R, Wr):
        op("v", lambda: v.tensor_tensor(out, in0, in1, o), R, Wr)

    def cp(out, in_, R, Wr):
        op("v", lambda: v.tensor_copy(out, in_), R, Wr)

    def ms(ap, c, Wr):
        op("v", lambda: v.memset(ap, c), [], Wr)

    def act(out, in_, R, Wr, func=None, **kw):
        op("a", lambda: a.activation(out, in_, AF.Identity if func is None else func, **kw), R, Wr)

    def mm(items, R, Wr, first=True, last=True):
        def fn():
            ins = None
            for n, (o, l, r) in enumerate(items):
                ins = pe.matmul(o, l, r, first and n == 0, last and n == len(items) - 1)
            return ins
        op("t", fn, R, Wr)

    def iota(out, pat, base, cm, Wr, small=True):
        if small:
            op("g", lambda: g.iota(out, pat, base, cm, allow_small_or_imprecise_dtypes=True), [], Wr)
        else:
            op("g", lambda: g.iota(out, pat, base, cm), [], Wr)

    def keep(out, in_, pat, cmp, cm, R, Wr):
        op("g", lambda: g.affine_select(out, in_, pat, cmp, 0.0, 0, cm), R, Wr)

    def diagonal(buf, pat, base, key):
        iota(buf[:], pat, base, 0, [key])
        keep(buf[:], buf[:], [[-1, 128]], A.is_equal, 1, [key], [key])

    rt_all = [routes(T, topo, r) for r in range(N)]
    arrive = 0
    for r in range(N):
        if r != rank:
            h, e = rt_all[r][rank]
            arrive += len(e) if h == core else len(topo.engines(h, core))
    relayed = [q for q, (h, e) in rt_all[rank].items() if h != T.cores[q]]
    direct = [q for q, (h, e) in rt_all[rank].items() if h == T.cores[q]]
    order = [rank] + direct + relayed
    nls = [0, 0]

    def send(m, qs, src_of, keys_of):
        for run in in_calls(qs):
            trs = []
            for q in run:
                deps("g", keys_of(q), [])
                h, e = rt_all[rank][q]
                rid, pid = topo.addr(h, core)
                trs.append(RemoteDMATransfer(dst_ids=[DstId(rid=rid, pnc=pid)], dma_engine_mask=mask_of(e),
                                             remote_sem=T.sem["arr%d" % m], src=src_of(q), dst=landing(T, m, rank, q)))
                nls[min(m, 1)] += len(e)
            g.remote_dma_fused(trs, local_sem=T.sem.ls if m else T.sem.ls0)

    for m in range(8):
        key = "RL" if m == 1 else ("FL%d" % ((m - 2) // 2) if m >= 2 and m % 2 == 0 else "Dw%d.g" % (0 if m == 0 else (m - 1) // 2))
        lastw[key] = ("arr%d" % m, arrive, "x", True)
        cnt["arr%d" % m] = arrive
    Dw = [T["Dw%d" % t] for t in range(RO)]

    def part(buf, q, w):
        d = (q - rank) % N
        return buf[:, (d - 1) * w:d * w]

    def guests(t):
        Gs, own = T["Gs%d" % t], Dw[t][:, 0:V]
        if t == 0:
            for n, q in enumerate(relayed + direct):
                (act if n % 2 else cp)(part(Gs, q, G), own.indirect(part(T.SNU, q, 16)), ["Dw0.o", "SNU"], ["Gs0.%d" % q])
            for qs in (relayed, direct):
                send(0, qs, lambda q: part(Gs, q, G), lambda q: ["Gs0.%d" % q])
            return
        act(Gs[:], own.indirect(T.SNU[:]), ["Dw%d.o" % t, "SNU"], ["Gs%d" % t])
        for qs in (relayed, direct):
            send(1 + 2 * t, qs, lambda q: part(Gs, q, G), lambda q: ["Gs%d" % t])

    def selectors(lo, hi):
        for i in range(lo, hi):
            act(T.SI[:, 128 * i:128 * i + 128], T.BLK[:], ["BLK", "RM"], ["SI%d" % i], scale=T.RM[:, i:i + 1])

    dma("s", T.SNI[:], T.snd[:], [], ["SNI"])
    dma("a", Dw[0][:, 0:V], T.d0[:], [], ["Dw0.o"])
    dma("s", T.FLI[:], T.fl[:], [], ["FLI"])
    dma("s", Dw[0][:, 2560:2576], T.rt[:], [], ["Dw0.r"])
    dma("a", T.LABI[:], T.lab[:], [], ["LABI"])
    iota(T.pcol[:, 0:1], [[0, 1]], 0, 1, ["p0"], False)
    iota(T.vraw[:], [[1, 48]], 0, 48, ["vraw"], False)
    iota(T.MG[:], [[1, 8], [0, 16]], 0, 0, ["MG"])
    iota(T.IJ[:], [[1, 256]], 0, 0, ["IJ"])
    iota(T.praw[:], [[1, 16]], 0, 16, ["praw"], False)
    ms(T.VS[:], 0.0, ["VS"])
    ts(T.pcol[:, 1:2], T.pcol[:, 0:1], 4, A.arith_shift_right, ["p0"], ["p1"])
    ts(T.pcol[:, 2:3], T.pcol[:, 0:1], 15, A.bitwise_and, ["p0"], ["p2"])
    ms(T.ZB[:], 0.0, ["ZB"])
    cp(T.CF[:, 0:3], T.pcol[:, 0:3], ["p0", "p1", "p2"], ["CF"])
    pgf, prf = T.CF[:, 1:2], T.CF[:, 2:3]
    ms(T.CM[:, 0:V], 0.0, ["CM.o"])
    ts(T.CF[:, 4:5], pgf, 768.0, A.mult, ["CF"], ["CF4"])
    ts(T.BLK[:], T.MG[:], pgf, A.is_equal, ["MG", "CF"], ["BLK"])
    ts(T.vR[:], T.vraw[:], T.CF[:, 4:5], A.subtract, ["vraw", "CF4"], ["vR"])
    ts(T.RM[:], T.IJ[:, 0:16], prf, A.is_equal, ["IJ", "CF"], ["RM"])
    ts(T.t48a[:], T.vR[:], 15, A.bitwise_and, ["vR"], ["t48a"])
    ts(T.t48b[:], T.vR[:], 4, A.arith_shift_right, ["vR"], ["t48b"])
    ts(T.q0[:], T.t48a[:], 48.0, A.mult, ["t48a"], ["q0"], 48.0, A.add)
    ts(T.q1[:], T.t48b[:], 32.0, A.add, ["t48b"], ["q1"])
    ts(T.q2[:], T.ZB[:, 0:48], prf, A.add, ["ZB", "CF"], ["q2"], 192.0, A.mult)
    dma("s", T.VS[0::16, :], T.q0[:], ["q0", "VS"], ["VS.0"])
    dma("s", T.VS[1::16, :], T.q1[:], ["q1", "VS"], ["VS.1"])
    dma("s", T.CM[0::16, 0:V], T.q2[:], ["q2", "CM.o"], ["CM.0"])
    dma("s", T.CM[1::16, 0:V], T.IJ[:, 0:48], ["IJ", "CM.o"], ["CM.1"])
    dma("s", T.LD[:], T.ld[:], [], ["LD"])
    cp(T.SNU[:], T.SNI[:], ["SNI"], ["SNU"])
    keep(T.LT[:], T.BLK[:], [[1, 128]], A.is_gt, -1, ["BLK"], ["LT"])
    iota(T.ZS[:], [[0, 144]], 0, 0, ["ZS0"])
    for qs in (relayed, direct):
        send(1, qs, lambda q: part(T.SNI, q, 16), lambda q: ["SNI"])
    ts(T.c1[:], T.vR[:], -1.0, A.mult, ["vR"], ["c1"], 767.0, A.add)
    ts(T.c2[:], T.vR[:], -1.0, A.mult, ["vR"], ["c2"], 768.0, A.add)
    selectors(0, 4)
    guests(0)
    lastw["sent0"] = ("ls0", nls[0], "x", True)
    cnt["ls0"] = nls[0]
    dma("s", T.NBI[:], T.nb[:], ["sent0"], ["NBI"])
    dma("s", T.ND[:], T.nd[:], [], ["ND"])
    diagonal(T.ID, [[0, 128]], 1, "ID")
    iota(Dw[0][:, 2576:WP], [[0, 16]], 255, 0, ["Dw0.n"])
    cp(T.ZS[:, 15:143:16], T.BLK[:, 0:128:16], ["BLK", "ZS0"], ["ZS"])
    ts(T.CF[:, 6:7], T.RM[:, 0:1], float(TG), A.mult, ["RM"], ["CF6"])
    ts(T.CF[:, 7:8], T.RM[:, 3:4], float(TG // 2), A.mult, ["RM"], ["CF7"])
    ts(T.pr2[:], T.praw[:], 255, A.bitwise_and, ["praw"], ["pr2"])
    cp(T.bcf[:], T.IJ[:, 0:16], ["IJ"], ["bcf"])
    ts(T.CM[:, 2560:WP], T.IJ[:, 0:32], T.RM[:, 1:2], A.mult, ["IJ", "RM", "CF6"], ["CM.r"], T.CF[:, 6:7], A.add)
    cp(T.PERM[:], T.pr2[:], ["pr2"], ["PERM"])
    cp(T.BC[:], T.bcf[:], ["bcf"], ["BC"])
    for d in range(1, N):
        p = order.index((rank - d) % N)
        act(T.B48[:, d:d + 1], T.RM[:, 2:3], ["RM", "CF7"], ["B48.%d" % d], scale=48.0 * (p % 4),
            bias=T.CF[:, 7:8] if p >= 4 else 0.0)
    selectors(4, 16)
    iota(T.ZF[:], [[0, 384]], 0, 0, ["ZF"])
    iota(T.ZL[:], [[0, 272]], 0, 0, ["ZL0"])
    iota(T.ZD[:], [[0, 272]], 0, 0, ["ZD0"])
    iota(T.ONE[:], [[0, 128]], 1, 0, ["ONE"])
    diagonal(T.I16, [[0, 128]], -16, "I16")
    diagonal(T.I8K, [[0, 128]], -8192, "I8K")
    diagonal(T.I5, [[0, 128]], 512, "I5")
    diagonal(T.DK, [[0, 8], [-1, 16]], 0, "DK")
    iota(T.RS[:], [[0, 256]], -65536, 0, ["RS"])
    keep(T.RS[:], T.RS[:], [[0, 16], [1, 16]], A.is_equal, 0, ["RS"], ["RS"])
    for t in range(1, RO):
        iota(Dw[t][:, 2576:WP], [[0, 16]], 255, 0, ["Dw%d.n" % t])

    def sel(b):
        return T.ZS[:, 15 - b:143 - b]

    bank_at = [0]

    def min_chain(Gt, gk, lens, lk, n, old, ok, out, okeys, extra):
        acc = [T.aA, T.aB]
        groups = [[0], [1]] + [[i for i in (i0, i0 + 1) if i < n] for i0 in range(2, n, 2)]
        bks = [PSUM[(bank_at[0] + k) % 4] for k in range(len(groups))]
        bank_at[0] += len(groups)

        def spot(k, i):
            return T[bks[k]][:, 256 * (i % 2):256 * (i % 2) + 256]
        for k in range(2):
            items = [(spot(k, k), T.SI[:, 128 * k:128 * k + 128], lens[:])]
            if k == 0 and extra:
                items.append((spot(k, k), T.ID[:], T.INV[:]))
            mm(items, [lk, "ID", "SI%d" % k, "INV"], [bks[k]], last=False)
        for k, ii in enumerate(groups):
            for i in ii:
                items = [(spot(k, i), T.ID[:], Gt[:, i:4096:16])]
                if k >= 2:
                    items.insert(0, (spot(k, i), T.SI[:, 128 * i:128 * i + 128], lens[:]))
                mm(items, gk + [lk, "ID", "SI%d" % i], [bks[k]], first=k >= 2)
            for i in ii:
                ak = "acc%d" % (i % 2)
                if i < 2:
                    tt(acc[i][:], spot(k, i), old, A.min, ok, [bks[k], ak])
                elif i < n - 1:
                    tt(acc[i % 2][:], spot(k, i), acc[i % 2][:], A.min, [ak], [bks[k], ak])
                else:
                    tt(T.pa[:, 0:256], spot(k, i), acc[i % 2][:], A.min, [ak], [bks[k], "pa", "pa.x"])
        tt(out, T.pa[:, 0:256], acc[n % 2][:], A.min, ["pa.x", "acc%d" % (n % 2)], ["pa"] + okeys)

    for t in range(RO):
        last = t == RO - 1
        win = Dw[t][:, 0:WP]
        wk = ["Dw%d.o" % t, "Dw%d.g" % t, "Dw%d.r" % t, "Dw%d.n" % t]
        if t == 0:
            cp(T.F[:], T.FLI[:], ["FLI"], ["F"])
        else:
            FL, SM = T["FL%d" % (t - 1)], T["SM%d" % (t - 1)]
            mm([(T.pa[:, 0:48], T.ID[:], T.LEFT[:]), (T.pa[:, 0:48], T.ID[:], SM[:, 0:48])],
               ["ID", "LEFT", "SM%d.0" % (t - 1)], ["pa"], last=False)
            mm([(T.pa[:, 0:48], T.ID[:], FL[:, 48 * d:48 * d + 48]) for d in range(1, N)],
               ["FL%d" % (t - 1)], ["pa"], first=False)
            ts(T.F[:], T.pa[:, 0:48], THR[t - 1], A.is_ge, ["pa.x"], ["pa", "F"])
        op("v", lambda: v.tensor_tensor_scan(T.S[:], T.F[:], T.F[:], 0.0, A.add, A.max), ["F"], ["S"])
        mm([(T.pa[:, 64:65], T.LT[:], T.S[:, 47:48])], ["LT", "S"], ["pa"])
        mm([(T.pa[:, 65:66], T.BLK[:], T.S[:, 47:48])], ["BLK", "S"], ["pa"])
        tt(T.Fc[:], T.F[:], T.c2[:], A.mult, ["F", "c2"], ["Fc"])
        tt(T.Sc[:], T.S[:], T.c1[:], A.add, ["S", "c1"], ["Sc"])
        tt(T.pre[:], T.Sc[:], T.Fc[:], A.subtract, ["Sc", "Fc"], ["pre"])
        ts(T.POS[:], T.pre[:], T.pa[:, 64:65], A.add, ["pre", "pa.x"], ["pa", "POS"])
        k = CMP_A if t else 0
        cp(T.CW[:, 0:V].indirect(T.POS[:, k:48]), T.VS[:, 16 * k:V], ["POS", "VS", "VS.0", "VS.1"], ["CW"])
        if k:
            act(T.CWf[:, 0:V].indirect(T.POS[:, 0:k]), T.VSf[:], ["POS", "VSf"], ["CWf"], func=AF.Silu)
            act(T.CWa[:], T.CWf[:, 0:256], ["CWf"], ["CWa"])
        mm([(T.pb[:, 0:16], sel(b), T.CW[:, b:256:16]) for b in range(16)], ["ZS", "CW"], ["pb"], last=not k)
        if k:
            mm([(T.pb[:, 0:16], sel(b), T.CWa[:, b:256:16]) for b in range(16)], ["ZS", "CWa"], ["pb"], first=False)
        ts(T.INV[:], T.IJ[:], T.pa[:, 65:66], A.is_ge, ["IJ", "pa.x"], ["pa", "INV"], -512.0, A.mult)
        if not last:
            ts(T.lf0[:], T.S[:], T.pa[:, 64:65], A.add, ["S", "pa.x"], ["pa", "lf0"], 256.5, A.is_gt)
            tt(T.LEFT[:], T.lf0[:], T.F[:], A.mult, ["lf0", "F"], ["LEFT"])
        ts(T.TL[:], T.pb[:, 0:16], -80.0, A.add, [], ["pb", "TL"])
        cp(T.LO[:], T.LABI[:, 0:V].indirect(T.TL[:]), ["LABI", "TL"], ["LO"])
        if t == 0:
            cp(T.OLD[:], Dw[0][:, 0:V].indirect(T.TL[:]), ["Dw0.o", "TL"], ["OLD"])
            old, ok = T.OLD[:], ["OLD"]
            ms(T.VF[:], LEV[0], ["VF"])
            cp(T.RU[:], T.RL[:], ["RL"], ["RU"])
            for d in range(1, N):
                act(T.CM[:, V + (d - 1) * G:V + d * G], T.CM[:, 0:V].indirect(T.RU[:, 16 * (d - 1):16 * d]),
                    ["CM.0", "CM.1", "RU", "B48.%d" % d], ["CM.g%d" % d], bias=T.B48[:, d:d + 1])
        else:
            old, ok = T.Gl[:, 15:4096:16], ["Gl.a", "Gl.v"]
            cp(T.NO[:], T.NBI[:, 0:V].indirect(T.TL[:]), ["NBI", "TL"], ["NO"])
        act(T.LDT[:], T.LD[:, 0:V].indirect(T.TL[:]), ["LD", "TL"], ["LDT"])
        k = LAB_A[t]
        act(T.Gl[:, 0:16 * k], win.indirect(T.LO[:, 0:k]), wk + ["LO"], ["Gl.a"])
        if t == 0:
            cp(T.Gl[:, 16 * k:16 * k + 1280], win.indirect(T.LO[:, k:k + 80]), wk + ["LO"], ["Gl.w"])
            cp(T.NO[:], T.NBI[:, 0:V].indirect(T.TL[:]), ["NBI", "TL"], ["NO"])
            k += 80
        cp(T.Gl[:, 16 * k:4096], win.indirect(T.LO[:, k:256]), wk + ["LO"], ["Gl.v"])
        if not last:
            dma("s", Dw[t + 1][:, 0:V], Dw[t][:, 0:V], ["Dw%d.o" % t, "Gl.a"], ["Dw%d.o" % (t + 1)])
            dma("s", Dw[t + 1][:, 2560:2576], T.rt[:], [], ["Dw%d.r" % (t + 1)])
        else:
            dma("s", T.yl[:], T.YL[:], ["YL", "Gl.a"], ["yl"])
        act(T.NDT[:], T.ND[:, 0:V].indirect(T.TL[:]), ["ND", "TL"], ["NDT"])
        kn = 256 - NB_V[t]
        act(T.Gn[:, 0:16 * kn], win.indirect(T.NO[:, 0:kn]), wk + ["NO"], ["Gn"])
        if t == 0:
            dma("s", T.Wb[0::16, 0:TG], T.ZB[:], ["ZB"], ["Wb"])
            dma("s", T.Wf[0::16, 0:TG], T.ZF[:], ["ZF"], ["Wf"])
            dma("s", T.LABI[15::16, :], T.vR[:], ["vR"], ["LABI"])
            dma("s", T.LD[15::16, :], T.ZB[:, 0:48], ["ZB"], ["LD"])
        QQ = T.pa[:, 256:512]
        min_chain(T.Gl, ["Gl.a", "Gl.v"], T.LDT, "LDT", 12 + t, old, ok, QQ, ["QQ"], True)
        if kn < 256:
            cp(T.Gn[:, 16 * kn:4096], win.indirect(T.NO[:, kn:256]), wk + ["NO"], ["Gn.v"])
        if not last:
            ky = Y_V[t] // 16
            cuts = [0, ky] + [ky + (16 - ky) * c // 4 for c in range(1, 5)]
            for c in range(5):
                lo, hi = cuts[c], cuts[c + 1]
                if lo < hi:
                    (act if c else cp)(T.Y[:, 256 * lo:256 * hi], T.CM[:, 0:WP].indirect(T.NO[:, 16 * lo:16 * hi]),
                                       ["CM.0", "CM.1", "CM.g7", "CM.r", "NO"], ["Y%d" % c])
        min_chain(T.Gn, ["Gn", "Gn.v"], T.NDT, "NDT", 16, old, ok, T.CC[:], ["CC"], False)
        tt(T.NU[:], T.CC[:], QQ, A.is_ge, ["CC", "QQ"], ["pa", "NU"])
        nbk = PSUM[bank_at[0] % 4]
        bank_at[0] += 1

        def after_matmuls():
            o = T[nbk][:, 0:256]
            mm([(o, T.ID[:], T.CC[:]), (o, T.I5[:], T.NU[:])], ["ID", "I5", "CC", "NU"], [nbk])
            for h in range(2):
                o = T.pK[:, 128 * h:128 * h + 128]
                mm([(o, T.ONE[:], T.DK[:]), (o, T.CC[:, 128 * h:128 * h + 128], T.I16[:]),
                    (o, T.NU[:, 128 * h:128 * h + 128], T.I8K[:])], ["ONE", "DK", "CC", "NU", "I16", "I8K"], ["pK"])

        def label_rows():
            op("v", lambda: v.tensor_tensor_scan(T.KS[:], T.RS[:], T.pK[:, 0:256], 0.0, A.add, A.max), ["RS"], ["pK", "KS"])
            mk = T.KS[:, 15:256:16]
            ts(T.w0[:], mk, 4095.0, A.add, ["KS"], ["w0"], 0.0, A.max)
            ts(T.w3[:], mk, -4096.0, A.is_gt, ["KS"], ["w3"])
            ts(T.w2[:], T.w0[:], 15, A.bitwise_and, ["w0"], ["w2"])
            if not last:
                ts(T.w1[:], T.w0[:], 4, A.arith_shift_right, ["w0"], ["w1"])
            tt(T.ZL[:, 15:256:16], T.w2[:], T.w3[:], A.add, ["w2", "w3", "ZL0"], ["ZL"])
            for h in range(2):
                mm([(T.pK[:, 256 + 128 * h:384 + 128 * h], T.ZL[:, 128 * h + 3 - t:128 * h + 131 - t], T.ID[:])],
                   ["ZL", "ID"], ["pK"])
            if not last:
                cp(T.ZD[:, 15:256:16], T.w1[:], ["w1", "ZD0"], ["ZD"])
                for h in range(2):
                    mm([(T.pO[:, 256 + 128 * h:384 + 128 * h], T.ZD[:, 128 * h + 3 - t:128 * h + 131 - t], T.ID[:])],
                       ["ZD", "ID"], ["pO"])

        if last:
            after_matmuls()
            tt(T.n2[:], T[nbk][:, 0:256], old, A.min, ok, [nbk, "n2"])
            label_rows()
            cp(Dw[t][:, 0:V].indirect(T.TL[:]), T.n2[:], ["n2", "TL"], ["Dw%d.o" % t])
            dma("s", T.yd[:], Dw[t][:, 0:V], ["Dw%d.o" % t], ["yd"])
            act(T.LV[:], T.pK[:, 256:512], ["CF9"], ["pK", "LV"], scale=-1.0, bias=T.CF[:, 9:10])
            cp(T.YL[:, 0:V].indirect(T.TL[:]), T.LV[:], ["LV", "TL"], ["YL"])
            dma("a", T.yl[15::16, :], T.YL[15::16, :], ["YL"], ["yl"])
            break
        for c in range(5):
            if cuts[c] < cuts[c + 1]:
                mm([(T.pO[:, 0:256], sel(b), T.Y[:, 256 * b:256 * b + 256]) for b in range(cuts[c], cuts[c + 1])],
                   ["ZS", "Y%d" % c], ["pO"], first=cuts[c] == 0, last=c == 4)
        mm([(T.pb[:, 32:48], sel(b), T.NU[:, 16 * b:16 * b + 16]) for b in range(16)], ["ZS", "NU"], ["pb"])
        act(T.OS[:], T.pO[:, 0:256], [], ["pO", "OS"])
        if t == 0:
            act(T.VB[:], T.VF[:], ["VF"], ["VB"], func=AF.Silu)
        after_matmuls()
        ts(T.RED[:], T.pb[:, 32:48], 15.5, A.is_ge, [], ["pb", "RED"], float(BIG), A.mult)
        tt(T.TM[:], T.RED[:, 0:16].indirect(T.BC[:]), T.OS[:], A.add, ["RED", "BC", "OS"], ["TM"])
        cp(T.PO[:], T.TM[:, 0:256].indirect(T.PERM[:]), ["TM", "PERM"], ["PO"])
        for i in range(16):
            off = T.PO[:, 16 * i:16 * i + 16]
            if i < PUSH_A:
                act(T.Wf[:, 0:2 * BIG].indirect(off), T.VF[:], ["PO", "VF"], ["Wf"], func=AF.Silu)
            else:
                cp(T.Wb[:, 0:2 * BIG].indirect(off), T.VB[:], ["PO", "VB"], ["Wb"])
        for h in (1, 0):
            dma("a", T.stB[:, 192 * h:192 * h + 192], T.Wf[0::16, 3072 * h:3072 * h + 3072], ["Wf"], ["stB%d" % h])
            dma("s", T.stA[:, 192 * h:192 * h + 192], T.Wb[0::16, 3072 * h:3072 * h + 3072], ["Wb"], ["stA%d" % h])
        tt(T.n2[:], T[nbk][:, 0:256], old, A.min, ok, [nbk, "n2"])
        cp(Dw[t + 1][:, 0:V].indirect(T.TL[:]), T.n2[:], ["n2", "TL"], ["Dw%d.o" % (t + 1)])
        act(T.CWf[:, 0:256], T.ZB[:, 0:256], ["ZB"], ["CWf"])
        if t == 0:
            act(T.VSf[:], T.VS[:, 0:16 * CMP_A], ["VS", "VS.0", "VS.1"], ["VSf"])
        label_rows()
        SM = T["SM%d" % t]
        for h in (1, 0):
            tt(SM[:, 192 * h:192 * h + 192], T.stA[:, 192 * h:192 * h + 192], T.stB[:, 192 * h:192 * h + 192], A.max,
               ["stA%d" % h, "stB%d" % h], ["SM%d.%d" % (t, h)])
        for qs in (relayed, direct):
            send(2 + 2 * t, qs, lambda q: SM[:, 48 * order.index(q):48 * order.index(q) + 48],
                 lambda q: ["SM%d.%d" % (t, order.index(q) // 4)])
        guests(t + 1)
        if t == 0:
            cp(T.LA[:], T.LABI[:, 0:V].indirect(T.TL[:]), ["LABI", "TL"], ["LA"])
            cp(T.LDT[:], T.LD[:, 0:V].indirect(T.TL[:]), ["LD", "TL"], ["LDT"])
        else:
            cp(T.LA[:], T.LO[:], ["LO"], ["LA"])
        tt(T.DV[:], T.LDT[:], T.pO[:, 256:512], A.subtract, ["LDT"], ["pO", "DV"])
        tt(T.LV[:], T.LA[:], T.pK[:, 256:512], A.subtract, ["LA"], ["pK", "LV"])
        cp(T.LABI[:, 0:V].indirect(T.TL[:]), T.LV[:], ["LV", "TL"], ["LABI"])
        cp(T.LD[:, 0:V].indirect(T.TL[:]), T.DV[:], ["DV", "TL"], ["LD"])
        if t == 0:
            ts(T.CF[:, 8:9], T.RM[:, 15:16], -1.0, A.mult, ["RM"], ["CF8"], 1.0, A.add)
            ts(T.CF[:, 9:10], T.RM[:, 15:16], float(W - 1), A.mult, ["RM"], ["CF9"])
        ms(T.CW[:, 0:256], 0.0, ["CW"])
        if t + 2 < RO:
            ms(T.VF[:], LEV[t + 1], ["VF"])
            act(T.VB[:], T.VF[:], ["VF"], ["VB"], func=AF.Silu)
        else:
            ts(T.YL[:], T.LABI[:], T.CF[:, 8:9], A.mult, ["LABI", "CF8", "CF9"], ["YL"], T.CF[:, 9:10], A.add)
    g.wait_ge(T.sem.ls, nls[1])
    for sem, c in cnt.items():
        if max(waited[q].get(sem, 0) for q in Q) < c:
            g.wait_ge(T.sem[sem], c)
